import numpy as np
import ml_dtypes


def mxq(x, axis, fmt="e4m3"):
    dtype, down = {"e4m3": (ml_dtypes.float8_e4m3fn, 7), "e5m2": (ml_dtypes.float8_e5m2, 14)}[fmt]
    v = np.moveaxis(np.asarray(x, np.float32).astype(ml_dtypes.bfloat16).astype(np.float64), axis, -1)
    blocks = v.reshape(v.shape[:-1] + (-1, 32))
    amax = np.abs(blocks).max(-1, keepdims=True)
    byte = np.maximum(np.where(amax > 0, np.frexp(amax)[1] - 1 + 127, 0) - down, 1)
    scale = np.exp2(byte - 127.0)
    codes = (blocks / scale).astype(np.float32).astype(dtype).astype(np.float64)
    return np.moveaxis((codes * scale).reshape(v.shape), -1, axis)


WIDE = False


def mx_kscale(k):
    if not WIDE:
        return np.ones(k)
    levels = np.array([10, -10, 5, -5, 0])
    if k % 512:
        return np.exp2(np.random.permutation(np.resize(levels, k // 32))).repeat(32)
    a = np.empty((k // 512, 16))
    for p in range(k // 512):
        a[p, :8] = np.random.permutation(np.resize(levels, 8))
        for g in range(8):
            far = levels[np.abs(levels - a[p, g]) >= 10]
            a[p, g + 8] = far[np.random.randint(len(far))]
    return np.exp2(a.ravel()).repeat(32)


def f64(x):
    return np.asarray(x).astype(np.float64)


def striped(idx):
    return np.tile(np.asarray(idx).reshape(-1, 16).T, (8, 1)).astype(np.uint16)


def unstriped(offs):
    return offs[:16].T.reshape(-1).astype(np.int64)


E2M1 = np.array([0.0, 0.5, 1.0, 1.5, 2.0, 3.0, 4.0, 6.0, -0.0, -0.5, -1.0, -1.5, -2.0, -3.0, -4.0, -6.0])


def pack_weight(w, fmt):
    k, n = w.shape
    w = f64(np.asarray(w, np.float32).astype(ml_dtypes.bfloat16)).reshape(k // 32, 32, n)
    amax = np.abs(w).max(1)
    if fmt == "e4m3":
        byte = np.frexp(amax)[1] - 1 + 127 - 7
    else:
        mant, ex = np.frexp(amax / 6.0)
        byte = np.where(mant > 0.5, ex, ex - 1) + 127
    byte = np.clip(np.where(amax > 0, byte, 1), 1, 254)
    scaled = (w * np.exp2(127.0 - byte)[:, None, :]).reshape(k, n).astype(np.float32)
    by_word = np.ascontiguousarray(scaled.reshape(k // 512, 128, 4, n).transpose(0, 1, 3, 2))
    if fmt == "e4m3":
        words = by_word.astype(ml_dtypes.float8_e4m3fn).view(np.uint8)
    else:
        c = by_word.astype(ml_dtypes.float4_e2m1fn).view(np.uint8) & 0xF
        words = (c[..., 0::2] | (c[..., 1::2] << 4)).reshape(k // 512, 128, 2 * n)
    return np.ascontiguousarray(words), np.ascontiguousarray(byte.astype(np.uint8).reshape(k // 512, 16, n))


def unpack_weight(words, scales, fmt):
    g, _, n = scales.shape
    words = np.ascontiguousarray(words).reshape(g, 128, n, -1)
    if fmt == "e4m3":
        vals = words.view(ml_dtypes.float8_e4m3fn).astype(np.float64)
    else:
        nib = np.empty((g, 128, n, 4), np.uint8)
        nib[..., 0::2] = words & 0xF
        nib[..., 1::2] = words >> 4
        vals = E2M1[nib]
    vals = vals * np.repeat(np.exp2(scales.astype(np.float64) - 127.0), 8, axis=1)[..., None]
    return vals.transpose(0, 1, 3, 2).reshape(g * 512, n)


K, T, J, N, I, L = 1024, 1024, 512, 512, 512, 512


def setup_inputs():
    n = np.random.standard_normal
    idx = np.random.permutation(T)[:J]
    idx2 = np.random.permutation(T)[:I]
    fk = mx_kscale(K)
    fl = mx_kscale(L)
    xqp = pack_weight(n((K, T)) / fk[:, None], "e2m1")
    wap = pack_weight(n((K, N)) * 1 / np.sqrt(K) * fk[:, None], "e2m1")
    rqp = pack_weight(n((K, J)) * 0.3 / fk[:, None], "e4m3")
    wrp = pack_weight(n((K, N)) * 1 / np.sqrt(K) * fk[:, None], "e4m3")
    wcp = pack_weight(n((L, N)) * 1 / np.sqrt(L) * fl[:, None], "e4m3")
    return {
        "xq_words": xqp[0],
        "xq_scales": xqp[1],
        "wa_words": wap[0],
        "wa_scales": wap[1],
        "rq_words": rqp[0],
        "rq_scales": rqp[1],
        "wr_words": wrp[0],
        "wr_scales": wrp[1],
        "cx": (n((L, I)) / fl[:, None]).astype(np.float32),
        "wc_words": wcp[0],
        "wc_scales": wcp[1],
        "offs": striped(idx),
        "offs2": striped(idx2),
    }


def reference(xq_words, xq_scales, wa_words, wa_scales, rq_words, rq_scales, wr_words, wr_scales, cx, wc_words, wc_scales, offs, offs2):
    idx = unstriped(offs)
    idx2 = unstriped(offs2)
    xqu = unpack_weight(xq_words, xq_scales, "e2m1")
    wau = unpack_weight(wa_words, wa_scales, "e2m1")
    rqu = unpack_weight(rq_words, rq_scales, "e4m3")
    wru = unpack_weight(wr_words, wr_scales, "e4m3")
    wcu = unpack_weight(wc_words, wc_scales, "e4m3")
    z = wau.T @ xqu
    p = wru.T @ rqu
    cxq = mxq(f64(cx), 0, "e4m3")
    q = wcu.T @ cxq
    pg = np.zeros((N, T))
    pg[:, idx] = p
    qt = np.tanh(q)
    qg = np.zeros((N, T))
    qg[:, idx2] = qt
    y = z + pg + qg
    return y

@@ -1,0 +1,216 @@
+from contextlib import ExitStack
+
+import concourse.mybir as mybir
+
+K, T, J, N, I, L = 1024, 1024, 512, 512, 512, 512
+FLOPS = 2 * N * (K * T + K * J + L * I)
+
+F32 = mybir.dt.float32
+BF16 = mybir.dt.bfloat16
+I32 = mybir.dt.int32
+U32 = mybir.dt.uint32
+U16 = mybir.dt.uint16
+U8 = mybir.dt.uint8
+FP8X4 = mybir.dt.float8_e4m3fn_x4
+FP4X4 = mybir.dt.float4_e2m1fn_x4
+TANH = mybir.ActivationFunctionType.Tanh
+ADD = mybir.AluOpType.add
+
+P = 128
+BANK = 512
+BLOCKS = N // P
+PASSES = K // 512
+HEAD = 128
+REST = I - HEAD
+
+
+def tile_list_token_patches_two_kernel(tc, xq_words, xq_scales, wa_words, wa_scales, rq_words, rq_scales,
+                                          wr_words, wr_scales, cx, wc_words, wc_scales, offs, offs2, out):
+    nc = tc.nc
+    with ExitStack() as ctx:
+        sb = ctx.enter_context(tc.tile_pool(name="sb", bufs=1))
+        ps = ctx.enter_context(tc.psum_pool(name="ps", bufs=1))
+
+        def tile(shape, dtype, name, after=None):
+            return sb.tile(shape, dtype, name=name, tag=after or name, align_bytes=64)
+
+        banks = [ps.tile([P, BANK], F32, name=f"bank{b}") for b in range(6)]
+        pq_banks, z_banks = banks[0:2], banks[2:6]
+
+        p_list = sb.tile([P, J // 16], U16, name="p_list")
+        q_list = sb.tile([P, I // 16], U16, name="q_list")
+
+        cx_rows = cx.rearrange("(p j) i -> p j i", j=4)
+        cx_head = tile([P, 4, HEAD], F32, "cx_head")
+        cx_rest = tile([P, 4, REST], F32, "cx_rest")
+        wc = tile([P, N], U32, "wc")
+        wc_sc = tile([P, N], U8, "wc_sc")
+        rq = tile([P, PASSES, J], U32, "rq")
+        wr = tile([P, PASSES, N], U32, "wr")
+        rq_sc = tile([P, J], U8, "rq_sc")
+        wr_sc = tile([P, N], U8, "wr_sc")
+        xq = tile([P, PASSES, 2 * T], U8, "xq")
+        wa = tile([P, PASSES, 2 * N], U8, "wa")
+        q_page = [tile([P, T], F32, f"q_page{b}") for b in range(2)]
+        xq_sc = tile([P, PASSES * T], U8, "xq_sc")
+        wa_sc = tile([P, PASSES * N], U8, "wa_sc")
+        warm = tile([P, 8], F32, "warm")
+        warm_out = tile([P, 8], F32, "warm_out")
+
+        def load_scales_side_by_side(queue, plane, scales):
+            passes = scales.shape[0]
+            rows = scales.bitcast(I32).rearrange("z (q r) c -> r q z c", r=4)
+            view = plane[:].bitcast(I32)
+            for r in range(4):
+                queue.dma_start(out=view[r:P:32, :].rearrange("q (z c) -> q z c", z=passes), in_=rows[r])
+
+        def load_scales_stacked(plane, scales):
+            rows = scales.bitcast(I32)
+            view = plane[:].bitcast(I32)
+            for q in range(4):
+                nc.sync.dma_start(out=view[32 * q : 32 * q + 4 * PASSES, :], in_=rows[:, 4 * q : 4 * q + 4, :])
+
+        def fp8_words(words):
+            return words.rearrange("z p c t -> p z (c t)").bitcast(I32)
+
+        def fp4_words(words):
+            return words.rearrange("z p c -> p z c").bitcast(I32)
+
+        nc.gpsimd.memset(wc_sc[:].bitcast(I32), 0)
+        nc.sync.dma_start(out=cx_head[:], in_=cx_rows[:, :, 0:HEAD])
+        nc.sync.dma_start(out=wc[:].bitcast(I32), in_=fp8_words(wc_words)[:, 0, :])
+        load_scales_side_by_side(nc.sync, wc_sc, wc_scales)
+        nc.sync.dma_start(q_list[:], offs2)
+        nc.sync.dma_start(out=cx_rest[:], in_=cx_rows[:, :, HEAD:I])
+        nc.vector.memset(warm[:], 0.0)
+        nc.scalar.activation(out=warm_out[:], in_=warm[:], func=TANH)
+        nc.gpsimd.memset(rq_sc[:].bitcast(I32), 0)
+        nc.gpsimd.memset(wr_sc[:].bitcast(I32), 0)
+        load_scales_stacked(rq_sc, rq_scales)
+        load_scales_stacked(wr_sc, wr_scales)
+        nc.sync.dma_start(out=rq[:].bitcast(I32), in_=fp8_words(rq_words))
+        nc.sync.dma_start(out=wr[:].bitcast(I32), in_=fp8_words(wr_words))
+        nc.sync.dma_start(p_list[:], offs)
+        for page in q_page:
+            nc.vector.memset(page[:], 0.0)
+        nc.vector.memset(wa_sc[:].bitcast(I32), 0)
+        nc.vector.memset(xq_sc[:].bitcast(I32), 0)
+
+        def interleave(copy, dst, src):
+            copy(out=dst.rearrange("p (c i t) -> p c t i", i=4, t=4), in_=src.rearrange("p t (c i) -> p c t i", i=4))
+
+        head_bf = tile([P, 4 * HEAD], BF16, "head_bf")
+        head_codes = tile([P, HEAD], U32, "head_codes")
+        head_sc = tile([P, HEAD], U8, "head_sc")
+        interleave(nc.vector.tensor_copy, head_bf[:], cx_head[:])
+        nc.vector.quantize_mx(out=head_codes[:].bitcast(FP8X4), scales=head_sc[:], in_=head_bf[:])
+        q_page.append(tile([P, T], F32, "q_page2", after="head_bf"))
+        nc.vector.memset(q_page[2][:], 0.0)
+
+        def wc_block(b):
+            return wc[:, b * P : (b + 1) * P].bitcast(FP8X4), wc_sc[:, b * P : (b + 1) * P]
+
+        def context_product(dst, b, codes, scales):
+            words, w_scales = wc_block(b)
+            nc.tensor.matmul_mx(out=dst, lhsT=words, lhsT_scale=w_scales, rhs=codes.bitcast(FP8X4), rhs_scale=scales,
+                                start=True, stop=True)
+
+        head_list = q_list[:, 0 : HEAD // 16]
+        rest_list = q_list[:, HEAD // 16 : I // 16]
+        qt_head0 = tile([P, HEAD], F32, "qt_head0")
+        qt_head = tile([P, (BLOCKS - 1) * HEAD], F32, "qt_head")
+        context_product(pq_banks[0][:, 0:HEAD], 0, head_codes[:], head_sc[:])
+        nc.scalar.activation(out=qt_head0[:], in_=pq_banks[0][:, 0:HEAD], func=TANH)
+        nc.vector.tensor_copy(out=q_page[0][:].indirect(head_list), in_=qt_head0[:])
+        for b in range(1, BLOCKS):
+            context_product(pq_banks[1][:, (b - 1) * HEAD : b * HEAD], b, head_codes[:], head_sc[:])
+        nc.scalar.activation(out=qt_head[:], in_=pq_banks[1][:, 0 : (BLOCKS - 1) * HEAD], func=TANH)
+
+        def scatter_head(b):
+            nc.vector.tensor_copy(out=q_page[b][:].indirect(head_list), in_=qt_head[:, (b - 1) * HEAD : b * HEAD])
+
+        for b in range(1, BLOCKS - 1):
+            scatter_head(b)
+
+        p_page = [tile([P, T], F32, "p_page0", after="head_codes"), tile([P, T], F32, "p_page1", after="qt_head0")]
+        nc.gpsimd.memset(p_page[0][:], 0.0)
+        load_scales_side_by_side(nc.gpsimd, wa_sc, wa_scales)
+        load_scales_side_by_side(nc.gpsimd, xq_sc, xq_scales)
+        nc.gpsimd.memset(p_page[1][:], 0.0)
+        nc.sync.dma_start(out=wa[:].bitcast(I32), in_=fp4_words(wa_words))
+        nc.sync.dma_start(out=xq[:].bitcast(I32), in_=fp4_words(xq_words))
+
+        p_vals = [tile([P, J], F32, f"p_vals{b}") for b in range(BLOCKS)]
+        qt_vals = [tile([P, REST], F32, f"qt_vals{b}") for b in range(BLOCKS)]
+        z_vals = [tile([P, T], F32, f"z_vals{b}") for b in range(BLOCKS)]
+        rest_bf = tile([P, 4 * REST], BF16, "rest_bf")
+        rest_codes = tile([P, REST], U32, "rest_codes")
+        rest_sc = tile([P, REST], U8, "rest_sc")
+        rest_parts = [(0, 256), (256, REST)]
+
+        def make_p(b, parts):
+            cols = slice(b * P, (b + 1) * P)
+            width = J // len(parts)
+            for part, bank in enumerate(parts):
+                listed = slice(part * width, (part + 1) * width)
+                for z in range(PASSES):
+                    nc.tensor.matmul_mx(out=bank[:, 0:width], lhsT=wr[:, z, cols].bitcast(FP8X4),
+                                        lhsT_scale=wr_sc[4 * z : P, cols], rhs=rq[:, z, listed].bitcast(FP8X4),
+                                        rhs_scale=rq_sc[4 * z : P, listed], start=(z == 0), stop=(z == PASSES - 1))
+                nc.scalar.copy(out=p_vals[b][:, listed], in_=bank[:, 0:width])
+
+        def make_qt(b, bank):
+            for lo, hi in rest_parts:
+                context_product(bank[:, lo:hi], b, rest_codes[:, lo:hi], rest_sc[:, lo:hi])
+            nc.scalar.activation(out=qt_vals[b][:], in_=bank[:, 0:REST], func=TANH)
+
+        def make_z(b):
+            for h, bank in enumerate(z_banks[2 * (b % 2) : 2 * (b % 2) + 2]):
+                for z in range(PASSES):
+                    nc.tensor.matmul_mx(
+                        out=bank[:],
+                        lhsT=wa[:, z, 2 * b * P : 2 * (b + 1) * P].bitcast(FP4X4),
+                        lhsT_scale=wa_sc[:, z * N + b * P : z * N + (b + 1) * P],
+                        rhs=xq[:, z, 2 * h * BANK : 2 * (h + 1) * BANK].bitcast(FP4X4),
+                        rhs_scale=xq_sc[:, z * T + h * BANK : z * T + (h + 1) * BANK],
+                        start=(z == 0), stop=(z == PASSES - 1))
+                nc.scalar.copy(out=z_vals[b][:, h * BANK : (h + 1) * BANK], in_=bank[:])
+
+        def scatter_p(b):
+            nc.vector.tensor_copy(out=p_page[b % 3][:].indirect(p_list[:]), in_=p_vals[b][:])
+
+        def scatter_qt(b):
+            nc.vector.tensor_copy(out=q_page[b][:].indirect(rest_list), in_=qt_vals[b][:])
+
+        for c in range(REST // HEAD):
+            interleave(nc.scalar.copy, rest_bf[:, 4 * c * HEAD : 4 * (c + 1) * HEAD], cx_rest[:, :, c * HEAD : (c + 1) * HEAD])
+        for lo, hi in rest_parts:
+            nc.vector.quantize_mx(out=rest_codes[:, lo:hi].bitcast(FP8X4), scales=rest_sc[:, lo:hi],
+                                  in_=rest_bf[:, 4 * lo : 4 * hi])
+        q_page.append(tile([P, T], F32, "q_page_last", after="rest_bf"))
+        nc.vector.memset(q_page[-1][:], 0.0)
+        scatter_head(BLOCKS - 1)
+        p_page.append(tile([P, T], F32, "p_page2", after="qt_head"))
+        nc.gpsimd.memset(p_page[2][:], 0.0)
+        last = BLOCKS - 1
+        for b in range(BLOCKS):
+            make_qt(b, pq_banks[0])
+            scatter_qt(b)
+            make_p(b, pq_banks[0:1])
+            if b < last:
+                scatter_p(b)
+            make_z(b)
+        for b in range(BLOCKS):
+            zq = tile([P, T], F32, "zq")
+            nc.gpsimd.tensor_tensor(out=zq[:], in0=z_vals[b][:], in1=q_page[b][:], op=ADD)
+            rows = slice(b * P, (b + 1) * P)
+            if b < last:
+                result = tile([P, T], F32, f"result{b}")
+                nc.gpsimd.tensor_tensor(out=result[:], in0=zq[:], in1=p_page[b][:], op=ADD)
+                nc.sync.dma_start(out=out[rows, :], in_=result[:])
+            if b == 0:
+                scatter_p(last)
+        for lo, hi, queue in ((0, 512, nc.sync), (512, 768, nc.scalar), (768, 1024, nc.sync)):
+            result = tile([P, hi - lo], F32, f"result_last{lo}")
+            nc.vector.tensor_tensor(out=result[:], in0=zq[:, lo:hi], in1=p_page[last % 3][:, lo:hi], op=ADD)
+            queue.dma_start(out=out[rows, lo:hi], in_=result[:])

@@ -34,8 +34,8 @@ def tile_list_token_patches_two_kernel(tc, xq_words, xq_scales, wa_words, wa_sca
         def tile(shape, dtype, name, after=None):
             return sb.tile(shape, dtype, name=name, tag=after or name, align_bytes=64)
 
-        banks = [ps.tile([P, BANK], F32, name=f"bank{b}") for b in range(6)]
-        pq_banks, z_banks = banks[0:2], banks[2:6]
+        banks = [ps.tile([P, BANK], F32, name=f"bank{b}") for b in range(2)]
+        pq_banks = banks
 
         p_list = sb.tile([P, J // 16], U16, name="p_list")
         q_list = sb.tile([P, I // 16], U16, name="q_list")
@@ -134,11 +134,11 @@ def tile_list_token_patches_two_kernel(tc, xq_words, xq_scales, wa_words, wa_sca
 
         p_page = [tile([P, T], F32, "p_page0", after="head_codes"), tile([P, T], F32, "p_page1", after="qt_head0")]
         nc.gpsimd.memset(p_page[0][:], 0.0)
-        load_scales_side_by_side(nc.gpsimd, wa_sc, wa_scales)
-        load_scales_side_by_side(nc.gpsimd, xq_sc, xq_scales)
         nc.gpsimd.memset(p_page[1][:], 0.0)
         nc.sync.dma_start(out=wa[:].bitcast(I32), in_=fp4_words(wa_words))
         nc.sync.dma_start(out=xq[:].bitcast(I32), in_=fp4_words(xq_words))
+        load_scales_side_by_side(nc.sync, wa_sc, wa_scales)
+        load_scales_side_by_side(nc.sync, xq_sc, xq_scales)
 
         p_vals = [tile([P, J], F32, f"p_vals{b}") for b in range(BLOCKS)]
         qt_vals = [tile([P, REST], F32, f"qt_vals{b}") for b in range(BLOCKS)]
@@ -164,8 +164,8 @@ def tile_list_token_patches_two_kernel(tc, xq_words, xq_scales, wa_words, wa_sca
                 context_product(bank[:, lo:hi], b, rest_codes[:, lo:hi], rest_sc[:, lo:hi])
             nc.scalar.activation(out=qt_vals[b][:], in_=bank[:, 0:REST], func=TANH)
 
-        def make_z(b):
-            for h, bank in enumerate(z_banks[2 * (b % 2) : 2 * (b % 2) + 2]):
+        def make_z(b, halves):
+            for h, bank in enumerate(halves):
                 for z in range(PASSES):
                     nc.tensor.matmul_mx(
                         out=bank[:],
@@ -190,16 +190,19 @@ def tile_list_token_patches_two_kernel(tc, xq_words, xq_scales, wa_words, wa_sca
         q_page.append(tile([P, T], F32, "q_page_last", after="rest_bf"))
         nc.vector.memset(q_page[-1][:], 0.0)
         scatter_head(BLOCKS - 1)
-        p_page.append(tile([P, T], F32, "p_page2", after="qt_head"))
+        p_page.append(tile([P, T], F32, "p_page2", after="head_sc"))
         nc.gpsimd.memset(p_page[2][:], 0.0)
         last = BLOCKS - 1
+        make_qt(0, banks[0])
+        scatter_qt(0)
         for b in range(BLOCKS):
-            make_qt(b, pq_banks[0])
-            scatter_qt(b)
-            make_p(b, pq_banks[0:1])
+            here, other = banks[(b + 1) % 2], banks[b % 2]
+            make_p(b, [here])
             if b < last:
                 scatter_p(b)
-            make_z(b)
+                make_qt(b + 1, here)
+                scatter_qt(b + 1)
+            make_z(b, [other, here])
         for b in range(BLOCKS):
             zq = tile([P, T], F32, "zq")
             nc.gpsimd.tensor_tensor(out=zq[:], in0=z_vals[b][:], in1=q_page[b][:], op=ADD)

@@ -21,6 +21,8 @@ BANK = 512
 BLOCKS = N // P
 PASSES = K // 512
 HEAD = 128
+MID = 128
+LATE = I - HEAD - MID
 REST = I - HEAD
 
 
@@ -35,14 +37,14 @@ def tile_list_token_patches_two_kernel(tc, xq_words, xq_scales, wa_words, wa_sca
             return sb.tile(shape, dtype, name=name, tag=after or name, align_bytes=64)
 
         banks = [ps.tile([P, BANK], F32, name=f"bank{b}") for b in range(2)]
-        pq_banks = banks
 
         p_list = sb.tile([P, J // 16], U16, name="p_list")
         q_list = sb.tile([P, I // 16], U16, name="q_list")
 
         cx_rows = cx.rearrange("(p j) i -> p j i", j=4)
         cx_head = tile([P, 4, HEAD], F32, "cx_head")
-        cx_rest = tile([P, 4, REST], F32, "cx_rest")
+        cx_mid = tile([P, 4, MID], F32, "cx_mid")
+        cx_late = tile([P, 4, LATE], F32, "cx_late")
         wc = tile([P, N], U32, "wc")
         wc_sc = tile([P, N], U8, "wc_sc")
         rq = tile([P, PASSES, J], U32, "rq")
@@ -51,7 +53,7 @@ def tile_list_token_patches_two_kernel(tc, xq_words, xq_scales, wa_words, wa_sca
         wr_sc = tile([P, N], U8, "wr_sc")
         xq = tile([P, PASSES, 2 * T], U8, "xq")
         wa = tile([P, PASSES, 2 * N], U8, "wa")
-        q_page = [tile([P, T], F32, f"q_page{b}") for b in range(2)]
+        q_page = {b: tile([P, T], F32, f"q_page{b}") for b in (1, 2)}
         xq_sc = tile([P, PASSES * T], U8, "xq_sc")
         wa_sc = tile([P, PASSES * N], U8, "wa_sc")
         warm = tile([P, 8], F32, "warm")
@@ -78,20 +80,23 @@ def tile_list_token_patches_two_kernel(tc, xq_words, xq_scales, wa_words, wa_sca
 
         nc.gpsimd.memset(wc_sc[:].bitcast(I32), 0)
         nc.sync.dma_start(out=cx_head[:], in_=cx_rows[:, :, 0:HEAD])
+        nc.sync.dma_start(out=cx_mid[:], in_=cx_rows[:, :, HEAD : HEAD + MID])
         nc.sync.dma_start(out=wc[:].bitcast(I32), in_=fp8_words(wc_words)[:, 0, :])
         load_scales_side_by_side(nc.sync, wc_sc, wc_scales)
         nc.sync.dma_start(q_list[:], offs2)
-        nc.sync.dma_start(out=cx_rest[:], in_=cx_rows[:, :, HEAD:I])
+        nc.sync.dma_start(out=cx_late[:], in_=cx_rows[:, :, HEAD + MID : I])
         nc.vector.memset(warm[:], 0.0)
         nc.scalar.activation(out=warm_out[:], in_=warm[:], func=TANH)
         nc.gpsimd.memset(rq_sc[:].bitcast(I32), 0)
         nc.gpsimd.memset(wr_sc[:].bitcast(I32), 0)
-        load_scales_stacked(rq_sc, rq_scales)
-        load_scales_stacked(wr_sc, wr_scales)
         nc.sync.dma_start(out=rq[:].bitcast(I32), in_=fp8_words(rq_words))
         nc.sync.dma_start(out=wr[:].bitcast(I32), in_=fp8_words(wr_words))
+        load_scales_stacked(rq_sc, rq_scales)
         nc.sync.dma_start(p_list[:], offs)
-        for page in q_page:
+        nc.sync.dma_start(out=wa[:].bitcast(I32), in_=fp4_words(wa_words))
+        nc.sync.dma_start(out=xq[:].bitcast(I32), in_=fp4_words(xq_words))
+        load_scales_stacked(wr_sc, wr_scales)
+        for page in q_page.values():
             nc.vector.memset(page[:], 0.0)
         nc.vector.memset(wa_sc[:].bitcast(I32), 0)
         nc.vector.memset(xq_sc[:].bitcast(I32), 0)
@@ -104,8 +109,13 @@ def tile_list_token_patches_two_kernel(tc, xq_words, xq_scales, wa_words, wa_sca
         head_sc = tile([P, HEAD], U8, "head_sc")
         interleave(nc.vector.tensor_copy, head_bf[:], cx_head[:])
         nc.vector.quantize_mx(out=head_codes[:].bitcast(FP8X4), scales=head_sc[:], in_=head_bf[:])
-        q_page.append(tile([P, T], F32, "q_page2", after="head_bf"))
-        nc.vector.memset(q_page[2][:], 0.0)
+        mid_bf = tile([P, 4 * MID], BF16, "mid_bf")
+        mid_codes = tile([P, MID], U32, "mid_codes", after="head_bf")
+        mid_sc = tile([P, MID], U8, "mid_sc")
+        interleave(nc.scalar.copy, mid_bf[:], cx_mid[:])
+        nc.vector.quantize_mx(out=mid_codes[:].bitcast(FP8X4), scales=mid_sc[:], in_=mid_bf[:])
+        q_page[3] = tile([P, T], F32, "q_page3", after="mid_bf")
+        nc.gpsimd.memset(q_page[3][:], 0.0)
 
         def wc_block(b):
             return wc[:, b * P : (b + 1) * P].bitcast(FP8X4), wc_sc[:, b * P : (b + 1) * P]
@@ -119,34 +129,31 @@ def tile_list_token_patches_two_kernel(tc, xq_words, xq_scales, wa_words, wa_sca
         rest_list = q_list[:, HEAD // 16 : I // 16]
         qt_head0 = tile([P, HEAD], F32, "qt_head0")
         qt_head = tile([P, (BLOCKS - 1) * HEAD], F32, "qt_head")
-        context_product(pq_banks[0][:, 0:HEAD], 0, head_codes[:], head_sc[:])
-        nc.scalar.activation(out=qt_head0[:], in_=pq_banks[0][:, 0:HEAD], func=TANH)
-        nc.vector.tensor_copy(out=q_page[0][:].indirect(head_list), in_=qt_head0[:])
-        for b in range(1, BLOCKS):
-            context_product(pq_banks[1][:, (b - 1) * HEAD : b * HEAD], b, head_codes[:], head_sc[:])
-        nc.scalar.activation(out=qt_head[:], in_=pq_banks[1][:, 0 : (BLOCKS - 1) * HEAD], func=TANH)
+        context_product(banks[0][:, 0:HEAD], 1, head_codes[:], head_sc[:])
+        nc.scalar.activation(out=qt_head0[:], in_=banks[0][:, 0:HEAD], func=TANH)
+        nc.vector.tensor_copy(out=q_page[1][:].indirect(head_list), in_=qt_head0[:])
+        head_cols = {b: slice(c * HEAD, (c + 1) * HEAD) for c, b in enumerate((2, 3, 0))}
+        for b, cols in head_cols.items():
+            context_product(banks[1][:, cols], b, head_codes[:], head_sc[:])
+        nc.scalar.activation(out=qt_head[:], in_=banks[1][:, 0 : (BLOCKS - 1) * HEAD], func=TANH)
 
         def scatter_head(b):
-            nc.vector.tensor_copy(out=q_page[b][:].indirect(head_list), in_=qt_head[:, (b - 1) * HEAD : b * HEAD])
+            nc.vector.tensor_copy(out=q_page[b][:].indirect(head_list), in_=qt_head[:, head_cols[b]])
 
-        for b in range(1, BLOCKS - 1):
-            scatter_head(b)
+        scatter_head(2)
+        scatter_head(3)
 
-        p_page = [tile([P, T], F32, "p_page0", after="head_codes"), tile([P, T], F32, "p_page1", after="qt_head0")]
+        p_page = [tile([P, T], F32, "p_page0", after="qt_head0")]
         nc.gpsimd.memset(p_page[0][:], 0.0)
-        nc.gpsimd.memset(p_page[1][:], 0.0)
-        nc.sync.dma_start(out=wa[:].bitcast(I32), in_=fp4_words(wa_words))
-        nc.sync.dma_start(out=xq[:].bitcast(I32), in_=fp4_words(xq_words))
         load_scales_side_by_side(nc.sync, wa_sc, wa_scales)
         load_scales_side_by_side(nc.sync, xq_sc, xq_scales)
 
         p_vals = [tile([P, J], F32, f"p_vals{b}") for b in range(BLOCKS)]
         qt_vals = [tile([P, REST], F32, f"qt_vals{b}") for b in range(BLOCKS)]
         z_vals = [tile([P, T], F32, f"z_vals{b}") for b in range(BLOCKS)]
-        rest_bf = tile([P, 4 * REST], BF16, "rest_bf")
-        rest_codes = tile([P, REST], U32, "rest_codes")
-        rest_sc = tile([P, REST], U8, "rest_sc")
-        rest_parts = [(0, 256), (256, REST)]
+        late_bf = tile([P, 4 * LATE], BF16, "late_bf")
+        late_codes = tile([P, LATE], U32, "late_codes")
+        late_sc = tile([P, LATE], U8, "late_sc")
 
         def make_p(b, parts):
             cols = slice(b * P, (b + 1) * P)
@@ -160,8 +167,8 @@ def tile_list_token_patches_two_kernel(tc, xq_words, xq_scales, wa_words, wa_sca
                 nc.scalar.copy(out=p_vals[b][:, listed], in_=bank[:, 0:width])
 
         def make_qt(b, bank):
-            for lo, hi in rest_parts:
-                context_product(bank[:, lo:hi], b, rest_codes[:, lo:hi], rest_sc[:, lo:hi])
+            context_product(bank[:, 0:MID], b, mid_codes[:], mid_sc[:])
+            context_product(bank[:, MID:REST], b, late_codes[:], late_sc[:])
             nc.scalar.activation(out=qt_vals[b][:], in_=bank[:, 0:REST], func=TANH)
 
         def make_z(b, halves):
@@ -182,19 +189,18 @@ def tile_list_token_patches_two_kernel(tc, xq_words, xq_scales, wa_words, wa_sca
         def scatter_qt(b):
             nc.vector.tensor_copy(out=q_page[b][:].indirect(rest_list), in_=qt_vals[b][:])
 
-        for c in range(REST // HEAD):
-            interleave(nc.scalar.copy, rest_bf[:, 4 * c * HEAD : 4 * (c + 1) * HEAD], cx_rest[:, :, c * HEAD : (c + 1) * HEAD])
-        for lo, hi in rest_parts:
-            nc.vector.quantize_mx(out=rest_codes[:, lo:hi].bitcast(FP8X4), scales=rest_sc[:, lo:hi],
-                                  in_=rest_bf[:, 4 * lo : 4 * hi])
-        q_page.append(tile([P, T], F32, "q_page_last", after="rest_bf"))
-        nc.vector.memset(q_page[-1][:], 0.0)
-        scatter_head(BLOCKS - 1)
-        p_page.append(tile([P, T], F32, "p_page2", after="head_sc"))
-        nc.gpsimd.memset(p_page[2][:], 0.0)
+        interleave(nc.scalar.copy, late_bf[:], cx_late[:])
+        nc.vector.quantize_mx(out=late_codes[:].bitcast(FP8X4), scales=late_sc[:], in_=late_bf[:])
+        q_page[0] = tile([P, T], F32, "q_page0", after="late_bf")
+        nc.vector.memset(q_page[0][:], 0.0)
+        scatter_head(0)
         last = BLOCKS - 1
         make_qt(0, banks[0])
         scatter_qt(0)
+        p_page.append(tile([P, T], F32, "p_page1", after="qt_head"))
+        p_page.append(tile([P, T], F32, "p_page2", after="qt_vals0"))
+        for page in p_page[1:]:
+            nc.gpsimd.memset(page[:], 0.0)
         for b in range(BLOCKS):
             here, other = banks[(b + 1) % 2], banks[b % 2]
             make_p(b, [here])

@@ -17,13 +17,18 @@ TANH = mybir.ActivationFunctionType.Tanh
 ADD = mybir.AluOpType.add
 
 P = 128
+PACK = 4
 BANK = 512
 BLOCKS = N // P
-PASSES = K // 512
-HEAD = 128
-MID = 128
-LATE = I - HEAD - MID
-REST = I - HEAD
+LAST = BLOCKS - 1
+PASSES = K // (P * PACK)
+GROUP = 16
+P_PAGES = BLOCKS - 1
+
+FIRST = 128
+SECOND = 128
+LATE = I - FIRST - SECOND
+REST = SECOND + LATE
 
 
 def tile_list_token_patches_two_kernel(tc, xq_words, xq_scales, wa_words, wa_scales, rq_words, rq_scales,
@@ -38,13 +43,13 @@ def tile_list_token_patches_two_kernel(tc, xq_words, xq_scales, wa_words, wa_sca
 
         banks = [ps.tile([P, BANK], F32, name=f"bank{b}") for b in range(2)]
 
-        p_list = sb.tile([P, J // 16], U16, name="p_list")
-        q_list = sb.tile([P, I // 16], U16, name="q_list")
+        p_list = sb.tile([P, J // GROUP], U16, name="p_list")
+        q_list = sb.tile([P, I // GROUP], U16, name="q_list")
 
-        cx_rows = cx.rearrange("(p j) i -> p j i", j=4)
-        cx_head = tile([P, 4, HEAD], F32, "cx_head")
-        cx_mid = tile([P, 4, MID], F32, "cx_mid")
-        cx_late = tile([P, 4, LATE], F32, "cx_late")
+        cx_rows = cx.rearrange("(p t) i -> p t i", t=PACK)
+        cx_first = tile([P, PACK, FIRST], F32, "cx_first")
+        cx_second = tile([P, PACK, SECOND], F32, "cx_second")
+        cx_late = tile([P, PACK, LATE], F32, "cx_late")
         wc = tile([P, N], U32, "wc")
         wc_sc = tile([P, N], U8, "wc_sc")
         rq = tile([P, PASSES, J], U32, "rq")
@@ -54,172 +59,165 @@ def tile_list_token_patches_two_kernel(tc, xq_words, xq_scales, wa_words, wa_sca
         xq = tile([P, PASSES, 2 * T], U8, "xq")
         wa = tile([P, PASSES, 2 * N], U8, "wa")
         q_page = {b: tile([P, T], F32, f"q_page{b}") for b in (1, 2)}
-        xq_sc = tile([P, PASSES * T], U8, "xq_sc")
-        wa_sc = tile([P, PASSES * N], U8, "wa_sc")
-        warm = tile([P, 8], F32, "warm")
-        warm_out = tile([P, 8], F32, "warm_out")
 
-        def load_scales_side_by_side(queue, plane, scales):
+        def load_scales_side_by_side(scale_tile, scales):
             passes = scales.shape[0]
-            rows = scales.bitcast(I32).rearrange("z (q r) c -> r q z c", r=4)
-            view = plane[:].bitcast(I32)
-            for r in range(4):
-                queue.dma_start(out=view[r:P:32, :].rearrange("q (z c) -> q z c", z=passes), in_=rows[r])
+            rows = scales.bitcast(I32).rearrange("a (q u) c -> u q a c", u=4)
+            view = scale_tile[:].bitcast(I32)
+            for u in range(4):
+                nc.sync.dma_start(out=view[u:P:32, :].rearrange("q (a c) -> q a c", a=passes), in_=rows[u])
 
-        def load_scales_stacked(plane, scales):
+        def load_scales_stacked(scale_tile, scales):
             rows = scales.bitcast(I32)
-            view = plane[:].bitcast(I32)
+            view = scale_tile[:].bitcast(I32)
             for q in range(4):
                 nc.sync.dma_start(out=view[32 * q : 32 * q + 4 * PASSES, :], in_=rows[:, 4 * q : 4 * q + 4, :])
 
         def fp8_words(words):
-            return words.rearrange("z p c t -> p z (c t)").bitcast(I32)
+            return words.rearrange("a p c t -> p a (c t)").bitcast(I32)
 
         def fp4_words(words):
-            return words.rearrange("z p c -> p z c").bitcast(I32)
+            return words.rearrange("a p c -> p a c").bitcast(I32)
 
         nc.gpsimd.memset(wc_sc[:].bitcast(I32), 0)
-        nc.sync.dma_start(out=cx_head[:], in_=cx_rows[:, :, 0:HEAD])
-        nc.sync.dma_start(out=cx_mid[:], in_=cx_rows[:, :, HEAD : HEAD + MID])
-        nc.sync.dma_start(out=wc[:].bitcast(I32), in_=fp8_words(wc_words)[:, 0, :])
-        load_scales_side_by_side(nc.sync, wc_sc, wc_scales)
+        nc.sync.dma_start(out=cx_first[:], in_=cx_rows[:, :, 0:FIRST])
+        load_scales_side_by_side(wc_sc, wc_scales)
         nc.sync.dma_start(q_list[:], offs2)
-        nc.sync.dma_start(out=cx_late[:], in_=cx_rows[:, :, HEAD + MID : I])
-        nc.vector.memset(warm[:], 0.0)
-        nc.scalar.activation(out=warm_out[:], in_=warm[:], func=TANH)
+        nc.sync.dma_start(out=cx_second[:], in_=cx_rows[:, :, FIRST : FIRST + SECOND])
+        nc.sync.dma_start(out=wc[:].bitcast(I32), in_=fp8_words(wc_words)[:, 0, :])
+        nc.sync.dma_start(out=cx_late[:], in_=cx_rows[:, :, FIRST + SECOND : I])
         nc.gpsimd.memset(rq_sc[:].bitcast(I32), 0)
         nc.gpsimd.memset(wr_sc[:].bitcast(I32), 0)
+        load_scales_stacked(rq_sc, rq_scales)
         nc.sync.dma_start(out=rq[:].bitcast(I32), in_=fp8_words(rq_words))
         nc.sync.dma_start(out=wr[:].bitcast(I32), in_=fp8_words(wr_words))
-        load_scales_stacked(rq_sc, rq_scales)
         nc.sync.dma_start(p_list[:], offs)
+        load_scales_stacked(wr_sc, wr_scales)
         nc.sync.dma_start(out=wa[:].bitcast(I32), in_=fp4_words(wa_words))
         nc.sync.dma_start(out=xq[:].bitcast(I32), in_=fp4_words(xq_words))
-        load_scales_stacked(wr_sc, wr_scales)
         for page in q_page.values():
             nc.vector.memset(page[:], 0.0)
-        nc.vector.memset(wa_sc[:].bitcast(I32), 0)
-        nc.vector.memset(xq_sc[:].bitcast(I32), 0)
 
         def interleave(copy, dst, src):
-            copy(out=dst.rearrange("p (c i t) -> p c t i", i=4, t=4), in_=src.rearrange("p t (c i) -> p c t i", i=4))
+            copy(out=dst.rearrange("p (c i t) -> p c t i", i=4, t=PACK),
+                 in_=src.rearrange("p t (c i) -> p c t i", i=4))
 
-        head_bf = tile([P, 4 * HEAD], BF16, "head_bf")
-        head_codes = tile([P, HEAD], U32, "head_codes")
-        head_sc = tile([P, HEAD], U8, "head_sc")
-        interleave(nc.vector.tensor_copy, head_bf[:], cx_head[:])
-        nc.vector.quantize_mx(out=head_codes[:].bitcast(FP8X4), scales=head_sc[:], in_=head_bf[:])
-        mid_bf = tile([P, 4 * MID], BF16, "mid_bf")
-        mid_codes = tile([P, MID], U32, "mid_codes", after="head_bf")
-        mid_sc = tile([P, MID], U8, "mid_sc")
-        interleave(nc.scalar.copy, mid_bf[:], cx_mid[:])
-        nc.vector.quantize_mx(out=mid_codes[:].bitcast(FP8X4), scales=mid_sc[:], in_=mid_bf[:])
-        q_page[3] = tile([P, T], F32, "q_page3", after="mid_bf")
+        first_bf = tile([P, PACK * FIRST], BF16, "first_bf")
+        first_codes = tile([P, FIRST], U32, "first_codes")
+        first_sc = tile([P, FIRST], U8, "first_sc")
+        interleave(nc.vector.tensor_copy, first_bf[:], cx_first[:])
+        wa_sc = tile([P, PASSES * N], U8, "wa_sc", after="cx_first")
+        nc.vector.memset(wa_sc[:].bitcast(I32), 0)
+        nc.vector.quantize_mx(out=first_codes[:].bitcast(FP8X4), scales=first_sc[:], in_=first_bf[:])
+        second_bf = tile([P, PACK * SECOND], BF16, "second_bf")
+        second_codes = tile([P, SECOND], U32, "second_codes", after="first_bf")
+        second_sc = tile([P, SECOND], U8, "second_sc")
+        interleave(nc.scalar.copy, second_bf[:], cx_second[:])
+        nc.vector.quantize_mx(out=second_codes[:].bitcast(FP8X4), scales=second_sc[:], in_=second_bf[:])
+        xq_sc = tile([P, PASSES * T], U8, "xq_sc", after="cx_second")
+        nc.vector.memset(xq_sc[:].bitcast(I32), 0)
+        q_page[3] = tile([P, T], F32, "q_page3", after="second_bf")
         nc.gpsimd.memset(q_page[3][:], 0.0)
 
-        def wc_block(b):
-            return wc[:, b * P : (b + 1) * P].bitcast(FP8X4), wc_sc[:, b * P : (b + 1) * P]
-
         def context_product(dst, b, codes, scales):
-            words, w_scales = wc_block(b)
-            nc.tensor.matmul_mx(out=dst, lhsT=words, lhsT_scale=w_scales, rhs=codes.bitcast(FP8X4), rhs_scale=scales,
-                                start=True, stop=True)
+            cols = slice(b * P, (b + 1) * P)
+            nc.tensor.matmul_mx(out=dst, lhsT=wc[:, cols].bitcast(FP8X4), lhsT_scale=wc_sc[:, cols],
+                                rhs=codes.bitcast(FP8X4), rhs_scale=scales, start=True, stop=True)
 
-        head_list = q_list[:, 0 : HEAD // 16]
-        rest_list = q_list[:, HEAD // 16 : I // 16]
-        qt_head0 = tile([P, HEAD], F32, "qt_head0")
-        qt_head = tile([P, (BLOCKS - 1) * HEAD], F32, "qt_head")
-        context_product(banks[0][:, 0:HEAD], 1, head_codes[:], head_sc[:])
-        nc.scalar.activation(out=qt_head0[:], in_=banks[0][:, 0:HEAD], func=TANH)
-        nc.vector.tensor_copy(out=q_page[1][:].indirect(head_list), in_=qt_head0[:])
-        head_cols = {b: slice(c * HEAD, (c + 1) * HEAD) for c, b in enumerate((2, 3, 0))}
-        for b, cols in head_cols.items():
-            context_product(banks[1][:, cols], b, head_codes[:], head_sc[:])
-        nc.scalar.activation(out=qt_head[:], in_=banks[1][:, 0 : (BLOCKS - 1) * HEAD], func=TANH)
+        first_list = q_list[:, 0 : FIRST // GROUP]
+        rest_list = q_list[:, FIRST // GROUP : I // GROUP]
+        qt_opening = tile([P, FIRST], F32, "qt_opening")
+        qt_first = tile([P, LAST * FIRST], F32, "qt_first")
+        context_product(banks[0][:, 0:FIRST], 1, first_codes[:], first_sc[:])
+        nc.scalar.activation(out=qt_opening[:], in_=banks[0][:, 0:FIRST], func=TANH)
+        nc.vector.tensor_copy(out=q_page[1][:].indirect(first_list), in_=qt_opening[:])
+        first_cols = {b: slice(c * FIRST, (c + 1) * FIRST) for c, b in enumerate((2, 3, 0))}
+        for b, cols in first_cols.items():
+            context_product(banks[1][:, cols], b, first_codes[:], first_sc[:])
+        nc.scalar.activation(out=qt_first[:], in_=banks[1][:, 0 : LAST * FIRST], func=TANH)
 
-        def scatter_head(b):
-            nc.vector.tensor_copy(out=q_page[b][:].indirect(head_list), in_=qt_head[:, head_cols[b]])
+        def scatter_first(b):
+            nc.vector.tensor_copy(out=q_page[b][:].indirect(first_list), in_=qt_first[:, first_cols[b]])
 
-        scatter_head(2)
-        scatter_head(3)
+        scatter_first(2)
+        scatter_first(3)
 
-        p_page = [tile([P, T], F32, "p_page0", after="qt_head0")]
+        p_page = [tile([P, T], F32, "p_page0", after="qt_opening")]
         nc.gpsimd.memset(p_page[0][:], 0.0)
-        load_scales_side_by_side(nc.sync, wa_sc, wa_scales)
-        load_scales_side_by_side(nc.sync, xq_sc, xq_scales)
+        load_scales_side_by_side(wa_sc, wa_scales)
+        load_scales_side_by_side(xq_sc, xq_scales)
 
         p_vals = [tile([P, J], F32, f"p_vals{b}") for b in range(BLOCKS)]
-        qt_vals = [tile([P, REST], F32, f"qt_vals{b}") for b in range(BLOCKS)]
+        qt_rest = [tile([P, REST], F32, f"qt_rest{b}") for b in range(BLOCKS)]
         z_vals = [tile([P, T], F32, f"z_vals{b}") for b in range(BLOCKS)]
-        late_bf = tile([P, 4 * LATE], BF16, "late_bf")
+        late_bf = tile([P, PACK * LATE], BF16, "late_bf")
         late_codes = tile([P, LATE], U32, "late_codes")
         late_sc = tile([P, LATE], U8, "late_sc")
 
-        def make_p(b, parts):
+        def make_p(b, bank):
             cols = slice(b * P, (b + 1) * P)
-            width = J // len(parts)
-            for part, bank in enumerate(parts):
-                listed = slice(part * width, (part + 1) * width)
-                for z in range(PASSES):
-                    nc.tensor.matmul_mx(out=bank[:, 0:width], lhsT=wr[:, z, cols].bitcast(FP8X4),
-                                        lhsT_scale=wr_sc[4 * z : P, cols], rhs=rq[:, z, listed].bitcast(FP8X4),
-                                        rhs_scale=rq_sc[4 * z : P, listed], start=(z == 0), stop=(z == PASSES - 1))
-                nc.scalar.copy(out=p_vals[b][:, listed], in_=bank[:, 0:width])
+            for a in range(PASSES):
+                nc.tensor.matmul_mx(out=bank[:], lhsT=wr[:, a, cols].bitcast(FP8X4), lhsT_scale=wr_sc[4 * a : P, cols],
+                                    rhs=rq[:, a, :].bitcast(FP8X4), rhs_scale=rq_sc[4 * a : P, :],
+                                    start=(a == 0), stop=(a == PASSES - 1))
+            nc.scalar.copy(out=p_vals[b][:], in_=bank[:])
 
-        def make_qt(b, bank):
-            context_product(bank[:, 0:MID], b, mid_codes[:], mid_sc[:])
-            context_product(bank[:, MID:REST], b, late_codes[:], late_sc[:])
-            nc.scalar.activation(out=qt_vals[b][:], in_=bank[:, 0:REST], func=TANH)
+        def make_qt_rest(b, bank):
+            context_product(bank[:, 0:SECOND], b, second_codes[:], second_sc[:])
+            context_product(bank[:, SECOND:REST], b, late_codes[:], late_sc[:])
+            nc.scalar.activation(out=qt_rest[b][:], in_=bank[:, 0:REST], func=TANH)
 
-        def make_z(b, halves):
-            for h, bank in enumerate(halves):
-                for z in range(PASSES):
+        def make_z(b, half_banks):
+            for h, bank in enumerate(half_banks):
+                for a in range(PASSES):
                     nc.tensor.matmul_mx(
                         out=bank[:],
-                        lhsT=wa[:, z, 2 * b * P : 2 * (b + 1) * P].bitcast(FP4X4),
-                        lhsT_scale=wa_sc[:, z * N + b * P : z * N + (b + 1) * P],
-                        rhs=xq[:, z, 2 * h * BANK : 2 * (h + 1) * BANK].bitcast(FP4X4),
-                        rhs_scale=xq_sc[:, z * T + h * BANK : z * T + (h + 1) * BANK],
-                        start=(z == 0), stop=(z == PASSES - 1))
+                        lhsT=wa[:, a, 2 * b * P : 2 * (b + 1) * P].bitcast(FP4X4),
+                        lhsT_scale=wa_sc[:, a * N + b * P : a * N + (b + 1) * P],
+                        rhs=xq[:, a, 2 * h * BANK : 2 * (h + 1) * BANK].bitcast(FP4X4),
+                        rhs_scale=xq_sc[:, a * T + h * BANK : a * T + (h + 1) * BANK],
+                        start=(a == 0), stop=(a == PASSES - 1))
                 nc.scalar.copy(out=z_vals[b][:, h * BANK : (h + 1) * BANK], in_=bank[:])
 
         def scatter_p(b):
-            nc.vector.tensor_copy(out=p_page[b % 3][:].indirect(p_list[:]), in_=p_vals[b][:])
+            nc.vector.tensor_copy(out=p_page[b % P_PAGES][:].indirect(p_list[:]), in_=p_vals[b][:])
 
-        def scatter_qt(b):
-            nc.vector.tensor_copy(out=q_page[b][:].indirect(rest_list), in_=qt_vals[b][:])
+        def scatter_qt_rest(b):
+            nc.vector.tensor_copy(out=q_page[b][:].indirect(rest_list), in_=qt_rest[b][:])
 
         interleave(nc.scalar.copy, late_bf[:], cx_late[:])
         nc.vector.quantize_mx(out=late_codes[:].bitcast(FP8X4), scales=late_sc[:], in_=late_bf[:])
         q_page[0] = tile([P, T], F32, "q_page0", after="late_bf")
         nc.vector.memset(q_page[0][:], 0.0)
-        scatter_head(0)
-        last = BLOCKS - 1
-        make_qt(0, banks[0])
-        scatter_qt(0)
-        p_page.append(tile([P, T], F32, "p_page1", after="qt_head"))
-        p_page.append(tile([P, T], F32, "p_page2", after="qt_vals0"))
+        scatter_first(0)
+        make_qt_rest(0, banks[0])
+        scatter_qt_rest(0)
+        p_page.append(tile([P, T], F32, "p_page1", after="qt_first"))
+        p_page.append(tile([P, T], F32, "p_page2", after="qt_rest0"))
         for page in p_page[1:]:
             nc.gpsimd.memset(page[:], 0.0)
+
         for b in range(BLOCKS):
-            here, other = banks[(b + 1) % 2], banks[b % 2]
-            make_p(b, [here])
-            if b < last:
+            p_bank, other_bank = banks[(b + 1) % 2], banks[b % 2]
+            make_p(b, p_bank)
+            if b < LAST:
                 scatter_p(b)
-                make_qt(b + 1, here)
-                scatter_qt(b + 1)
-            make_z(b, [other, here])
+                make_qt_rest(b + 1, p_bank)
+                scatter_qt_rest(b + 1)
+            make_z(b, [other_bank, p_bank])
+
         for b in range(BLOCKS):
             zq = tile([P, T], F32, "zq")
             nc.gpsimd.tensor_tensor(out=zq[:], in0=z_vals[b][:], in1=q_page[b][:], op=ADD)
-            rows = slice(b * P, (b + 1) * P)
-            if b < last:
+            if b < LAST:
                 result = tile([P, T], F32, f"result{b}")
                 nc.gpsimd.tensor_tensor(out=result[:], in0=zq[:], in1=p_page[b][:], op=ADD)
-                nc.sync.dma_start(out=out[rows, :], in_=result[:])
+                nc.sync.dma_start(out=out[b * P : (b + 1) * P, :], in_=result[:])
             if b == 0:
-                scatter_p(last)
-        for lo, hi, queue in ((0, 512, nc.sync), (512, 768, nc.scalar), (768, 1024, nc.sync)):
+                scatter_p(LAST)
+
+        pieces = ((0, T // 2, nc.sync), (T // 2, 3 * T // 4, nc.scalar), (3 * T // 4, T, nc.sync))
+        for lo, hi, queue in pieces:
             result = tile([P, hi - lo], F32, f"result_last{lo}")
-            nc.vector.tensor_tensor(out=result[:], in0=zq[:, lo:hi], in1=p_page[last % 3][:, lo:hi], op=ADD)
-            queue.dma_start(out=out[rows, lo:hi], in_=result[:])
+            nc.vector.tensor_tensor(out=result[:], in0=zq[:, lo:hi], in1=p_page[LAST % P_PAGES][:, lo:hi], op=ADD)
+            queue.dma_start(out=out[LAST * P : N, lo:hi], in_=result[:])

from contextlib import ExitStack

import concourse.mybir as mybir

K, T, J, N, I, L = 1024, 1024, 512, 512, 512, 512
FLOPS = 2 * N * (K * T + K * J + L * I)

F32 = mybir.dt.float32
BF16 = mybir.dt.bfloat16
I32 = mybir.dt.int32
U32 = mybir.dt.uint32
U16 = mybir.dt.uint16
U8 = mybir.dt.uint8
FP8X4 = mybir.dt.float8_e4m3fn_x4
FP4X4 = mybir.dt.float4_e2m1fn_x4
TANH = mybir.ActivationFunctionType.Tanh
ADD = mybir.AluOpType.add

P = 128
PACK = 4
BANK = 512
BLOCKS = N // P
LAST = BLOCKS - 1
PASSES = K // (P * PACK)
GROUP = 16
P_PAGES = BLOCKS - 1

FIRST = 128
SECOND = 128
LATE = I - FIRST - SECOND
REST = SECOND + LATE


def tile_list_token_patches_two_kernel(tc, xq_words, xq_scales, wa_words, wa_scales, rq_words, rq_scales,
                                          wr_words, wr_scales, cx, wc_words, wc_scales, offs, offs2, out):
    nc = tc.nc
    with ExitStack() as ctx:
        sb = ctx.enter_context(tc.tile_pool(name="sb", bufs=1))
        ps = ctx.enter_context(tc.psum_pool(name="ps", bufs=1))

        def tile(shape, dtype, name, after=None):
            return sb.tile(shape, dtype, name=name, tag=after or name, align_bytes=64)

        banks = [ps.tile([P, BANK], F32, name=f"bank{b}") for b in range(2)]

        p_list = sb.tile([P, J // GROUP], U16, name="p_list")
        q_list = sb.tile([P, I // GROUP], U16, name="q_list")

        cx_rows = cx.rearrange("(p t) i -> p t i", t=PACK)
        cx_first = tile([P, PACK, FIRST], F32, "cx_first")
        cx_second = tile([P, PACK, SECOND], F32, "cx_second")
        cx_late = tile([P, PACK, LATE], F32, "cx_late")
        wc = tile([P, N], U32, "wc")
        wc_sc = tile([P, N], U8, "wc_sc")
        rq = tile([P, PASSES, J], U32, "rq")
        wr = tile([P, PASSES, N], U32, "wr")
        rq_sc = tile([P, J], U8, "rq_sc")
        wr_sc = tile([P, N], U8, "wr_sc")
        xq = tile([P, PASSES, 2 * T], U8, "xq")
        wa = tile([P, PASSES, 2 * N], U8, "wa")
        q_page = {b: tile([P, T], F32, f"q_page{b}") for b in (1, 2)}

        def load_scales_side_by_side(scale_tile, scales):
            passes = scales.shape[0]
            rows = scales.bitcast(I32).rearrange("a (q u) c -> u q a c", u=4)
            view = scale_tile[:].bitcast(I32)
            for u in range(4):
                nc.sync.dma_start(out=view[u:P:32, :].rearrange("q (a c) -> q a c", a=passes), in_=rows[u])

        def load_scales_stacked(scale_tile, scales):
            rows = scales.bitcast(I32)
            view = scale_tile[:].bitcast(I32)
            for q in range(4):
                nc.sync.dma_start(out=view[32 * q : 32 * q + 4 * PASSES, :], in_=rows[:, 4 * q : 4 * q + 4, :])

        def fp8_words(words):
            return words.rearrange("a p c t -> p a (c t)").bitcast(I32)

        def fp4_words(words):
            return words.rearrange("a p c -> p a c").bitcast(I32)

        nc.gpsimd.memset(wc_sc[:].bitcast(I32), 0)
        nc.sync.dma_start(out=cx_first[:], in_=cx_rows[:, :, 0:FIRST])
        load_scales_side_by_side(wc_sc, wc_scales)
        nc.sync.dma_start(q_list[:], offs2)
        nc.sync.dma_start(out=cx_second[:], in_=cx_rows[:, :, FIRST : FIRST + SECOND])
        nc.sync.dma_start(out=wc[:].bitcast(I32), in_=fp8_words(wc_words)[:, 0, :])
        nc.sync.dma_start(out=cx_late[:], in_=cx_rows[:, :, FIRST + SECOND : I])
        nc.gpsimd.memset(rq_sc[:].bitcast(I32), 0)
        nc.gpsimd.memset(wr_sc[:].bitcast(I32), 0)
        load_scales_stacked(rq_sc, rq_scales)
        nc.sync.dma_start(out=rq[:].bitcast(I32), in_=fp8_words(rq_words))
        nc.sync.dma_start(out=wr[:].bitcast(I32), in_=fp8_words(wr_words))
        nc.sync.dma_start(p_list[:], offs)
        load_scales_stacked(wr_sc, wr_scales)
        nc.sync.dma_start(out=wa[:].bitcast(I32), in_=fp4_words(wa_words))
        nc.sync.dma_start(out=xq[:].bitcast(I32), in_=fp4_words(xq_words))
        for page in q_page.values():
            nc.vector.memset(page[:], 0.0)

        def interleave(copy, dst, src):
            copy(out=dst.rearrange("p (c i t) -> p c t i", i=4, t=PACK),
                 in_=src.rearrange("p t (c i) -> p c t i", i=4))

        first_bf = tile([P, PACK * FIRST], BF16, "first_bf")
        first_codes = tile([P, FIRST], U32, "first_codes")
        first_sc = tile([P, FIRST], U8, "first_sc")
        interleave(nc.vector.tensor_copy, first_bf[:], cx_first[:])
        wa_sc = tile([P, PASSES * N], U8, "wa_sc", after="cx_first")
        nc.vector.memset(wa_sc[:].bitcast(I32), 0)
        nc.vector.quantize_mx(out=first_codes[:].bitcast(FP8X4), scales=first_sc[:], in_=first_bf[:])
        second_bf = tile([P, PACK * SECOND], BF16, "second_bf")
        second_codes = tile([P, SECOND], U32, "second_codes", after="first_bf")
        second_sc = tile([P, SECOND], U8, "second_sc")
        interleave(nc.scalar.copy, second_bf[:], cx_second[:])
        nc.vector.quantize_mx(out=second_codes[:].bitcast(FP8X4), scales=second_sc[:], in_=second_bf[:])
        xq_sc = tile([P, PASSES * T], U8, "xq_sc", after="cx_second")
        nc.vector.memset(xq_sc[:].bitcast(I32), 0)
        q_page[3] = tile([P, T], F32, "q_page3", after="second_bf")
        nc.gpsimd.memset(q_page[3][:], 0.0)

        def context_product(dst, b, codes, scales):
            cols = slice(b * P, (b + 1) * P)
            nc.tensor.matmul_mx(out=dst, lhsT=wc[:, cols].bitcast(FP8X4), lhsT_scale=wc_sc[:, cols],
                                rhs=codes.bitcast(FP8X4), rhs_scale=scales, start=True, stop=True)

        first_list = q_list[:, 0 : FIRST // GROUP]
        rest_list = q_list[:, FIRST // GROUP : I // GROUP]
        qt_opening = tile([P, FIRST], F32, "qt_opening")
        qt_first = tile([P, LAST * FIRST], F32, "qt_first")
        context_product(banks[0][:, 0:FIRST], 1, first_codes[:], first_sc[:])
        nc.scalar.activation(out=qt_opening[:], in_=banks[0][:, 0:FIRST], func=TANH)
        nc.vector.tensor_copy(out=q_page[1][:].indirect(first_list), in_=qt_opening[:])
        first_cols = {b: slice(c * FIRST, (c + 1) * FIRST) for c, b in enumerate((2, 3, 0))}
        for b, cols in first_cols.items():
            context_product(banks[1][:, cols], b, first_codes[:], first_sc[:])
        nc.scalar.activation(out=qt_first[:], in_=banks[1][:, 0 : LAST * FIRST], func=TANH)

        def scatter_first(b):
            nc.vector.tensor_copy(out=q_page[b][:].indirect(first_list), in_=qt_first[:, first_cols[b]])

        scatter_first(2)
        scatter_first(3)

        p_page = [tile([P, T], F32, "p_page0", after="qt_opening")]
        nc.gpsimd.memset(p_page[0][:], 0.0)
        load_scales_side_by_side(wa_sc, wa_scales)
        load_scales_side_by_side(xq_sc, xq_scales)

        p_vals = [tile([P, J], F32, f"p_vals{b}") for b in range(BLOCKS)]
        qt_rest = [tile([P, REST], F32, f"qt_rest{b}") for b in range(BLOCKS)]
        z_vals = [tile([P, T], F32, f"z_vals{b}") for b in range(BLOCKS)]
        late_bf = tile([P, PACK * LATE], BF16, "late_bf")
        late_codes = tile([P, LATE], U32, "late_codes")
        late_sc = tile([P, LATE], U8, "late_sc")

        def make_p(b, bank):
            cols = slice(b * P, (b + 1) * P)
            for a in range(PASSES):
                nc.tensor.matmul_mx(out=bank[:], lhsT=wr[:, a, cols].bitcast(FP8X4), lhsT_scale=wr_sc[4 * a : P, cols],
                                    rhs=rq[:, a, :].bitcast(FP8X4), rhs_scale=rq_sc[4 * a : P, :],
                                    start=(a == 0), stop=(a == PASSES - 1))
            nc.scalar.copy(out=p_vals[b][:], in_=bank[:])

        def make_qt_rest(b, bank):
            context_product(bank[:, 0:SECOND], b, second_codes[:], second_sc[:])
            context_product(bank[:, SECOND:REST], b, late_codes[:], late_sc[:])
            nc.scalar.activation(out=qt_rest[b][:], in_=bank[:, 0:REST], func=TANH)

        def make_z(b, half_banks):
            for h, bank in enumerate(half_banks):
                for a in range(PASSES):
                    nc.tensor.matmul_mx(
                        out=bank[:],
                        lhsT=wa[:, a, 2 * b * P : 2 * (b + 1) * P].bitcast(FP4X4),
                        lhsT_scale=wa_sc[:, a * N + b * P : a * N + (b + 1) * P],
                        rhs=xq[:, a, 2 * h * BANK : 2 * (h + 1) * BANK].bitcast(FP4X4),
                        rhs_scale=xq_sc[:, a * T + h * BANK : a * T + (h + 1) * BANK],
                        start=(a == 0), stop=(a == PASSES - 1))
                nc.scalar.copy(out=z_vals[b][:, h * BANK : (h + 1) * BANK], in_=bank[:])

        def scatter_p(b):
            nc.vector.tensor_copy(out=p_page[b % P_PAGES][:].indirect(p_list[:]), in_=p_vals[b][:])

        def scatter_qt_rest(b):
            nc.vector.tensor_copy(out=q_page[b][:].indirect(rest_list), in_=qt_rest[b][:])

        interleave(nc.scalar.copy, late_bf[:], cx_late[:])
        nc.vector.quantize_mx(out=late_codes[:].bitcast(FP8X4), scales=late_sc[:], in_=late_bf[:])
        q_page[0] = tile([P, T], F32, "q_page0", after="late_bf")
        nc.vector.memset(q_page[0][:], 0.0)
        scatter_first(0)
        make_qt_rest(0, banks[0])
        scatter_qt_rest(0)
        p_page.append(tile([P, T], F32, "p_page1", after="qt_first"))
        p_page.append(tile([P, T], F32, "p_page2", after="qt_rest0"))
        for page in p_page[1:]:
            nc.gpsimd.memset(page[:], 0.0)

        for b in range(BLOCKS):
            p_bank, other_bank = banks[(b + 1) % 2], banks[b % 2]
            make_p(b, p_bank)
            if b < LAST:
                scatter_p(b)
                make_qt_rest(b + 1, p_bank)
                scatter_qt_rest(b + 1)
            make_z(b, [other_bank, p_bank])

        for b in range(BLOCKS):
            zq = tile([P, T], F32, "zq")
            nc.gpsimd.tensor_tensor(out=zq[:], in0=z_vals[b][:], in1=q_page[b][:], op=ADD)
            if b < LAST:
                result = tile([P, T], F32, f"result{b}")
                nc.gpsimd.tensor_tensor(out=result[:], in0=zq[:], in1=p_page[b][:], op=ADD)
                nc.sync.dma_start(out=out[b * P : (b + 1) * P, :], in_=result[:])
            if b == 0:
                scatter_p(LAST)

        pieces = ((0, T // 2, nc.sync), (T // 2, 3 * T // 4, nc.scalar), (3 * T // 4, T, nc.sync))
        for lo, hi, queue in pieces:
            result = tile([P, hi - lo], F32, f"result_last{lo}")
            nc.vector.tensor_tensor(out=result[:], in0=zq[:, lo:hi], in1=p_page[LAST % P_PAGES][:, lo:hi], op=ADD)
            queue.dma_start(out=out[LAST * P : N, lo:hi], in_=result[:])
